import numpy as np
CORES = [67,75,83,91,99,107,115,123]
N = 8
def setup_inputs(rng):
    return {"x": rng.standard_normal((N, 128 // N, 64), dtype=np.float32)}
def reference(x):
    g = np.concatenate(list(x), axis=0)
    return {"y": np.broadcast_to(g, (N,) + g.shape)}

@@ -1,0 +1,33 @@
+from concourse.bass import DstId, RemoteDMATransfer
+
+SCRATCH = {
+    "land": ("dram", [8, 128, 8], "float32"),
+}
+SEMAPHORES = ["loaded", "read", "arrived", "stored"]
+
+ENGINES = 0xFF
+NENG = 8
+
+
+def rank_program(g, core, T, topo):
+    rank = T.rank_of(core)
+    if rank is None:
+        return
+    others = [c for c in T.cores if c != core]
+
+    g.dma_start(T.land[rank], T.x[:]).then_inc(T.sem.loaded, 16)
+    g.wait_ge(T.sem.loaded, 16)
+
+    ids = []
+    for c in others:
+        rid, pid, se = topo.addr(c)
+        ids.append(DstId(rid=rid, pnc=pid))
+    g.remote_dma_fused(
+        [RemoteDMATransfer(dst_ids=ids, dma_engine_mask=ENGINES, remote_sem=T.sem.arrived,
+                           srcs=[T.land[rank]], dsts=[T.land[rank] for c in others])],
+        local_sem=T.sem.read)
+
+    g.wait_ge(T.sem.arrived, NENG * len(others))
+    g.dma_start(T.y[:], T.land[:]).then_inc(T.sem.stored, 16)
+    g.wait_ge(T.sem.read, NENG)
+    g.wait_ge(T.sem.stored, 16)

@@ -9,11 +9,28 @@ ENGINES = 0xFF
 NENG = 8
 
 
+def send_order(core, T, topo):
+    n = len(T.cores)
+    rank = T.rank_of(core)
+    here = topo.chip(core)
+    far, near, mate = [], [], []
+    for d in range(1, n):
+        c = T.cores[(rank + d) % n]
+        there = topo.chip(c)
+        if topo.mates(here, there):
+            mate.append(c)
+        elif topo.same_plane(here, there):
+            near.append(c)
+        else:
+            far.append(c)
+    return far + near + mate
+
+
 def rank_program(g, core, T, topo):
     rank = T.rank_of(core)
     if rank is None:
         return
-    others = [c for c in T.cores if c != core]
+    others = send_order(core, T, topo)
 
     g.dma_start(T.land[rank], T.x[:]).then_inc(T.sem.loaded, 16)
     g.wait_ge(T.sem.loaded, 16)

@@ -3,7 +3,7 @@ from concourse.bass import DstId, RemoteDMATransfer
 SCRATCH = {
     "land": ("dram", [8, 128, 8], "float32"),
 }
-SEMAPHORES = ["loaded", "read", "arrived", "stored"]
+SEMAPHORES = ["loaded", "read", "stored", "pair0", "pair1", "pair2", "pair3"]
 
 ENGINES = 0xFF
 NENG = 8
@@ -31,6 +31,10 @@ def rank_program(g, core, T, topo):
     if rank is None:
         return
     others = send_order(core, T, topo)
+    pair_sem = [T.sem.pair0, T.sem.pair1, T.sem.pair2, T.sem.pair3]
+    npairs = len(pair_sem)
+    mine = rank // 2
+    rows = T.y.shape[0] // npairs
 
     g.dma_start(T.land[rank], T.x[:]).then_inc(T.sem.loaded, 16)
     g.wait_ge(T.sem.loaded, 16)
@@ -40,11 +44,13 @@ def rank_program(g, core, T, topo):
         rid, pid, se = topo.addr(c)
         ids.append(DstId(rid=rid, pnc=pid))
     g.remote_dma_fused(
-        [RemoteDMATransfer(dst_ids=ids, dma_engine_mask=ENGINES, remote_sem=T.sem.arrived,
+        [RemoteDMATransfer(dst_ids=ids, dma_engine_mask=ENGINES, remote_sem=pair_sem[mine],
                            srcs=[T.land[rank]], dsts=[T.land[rank] for c in others])],
         local_sem=T.sem.read)
 
-    g.wait_ge(T.sem.arrived, NENG * len(others))
-    g.dma_start(T.y[:], T.land[:]).then_inc(T.sem.stored, 16)
+    for k in range(1, npairs + 1):
+        p = (mine - k) % npairs
+        g.wait_ge(pair_sem[p], NENG if p == mine else 2 * NENG)
+        g.dma_start(T.y[p * rows:(p + 1) * rows, :], T.land[2 * p:2 * p + 2]).then_inc(T.sem.stored, 16)
     g.wait_ge(T.sem.read, NENG)
-    g.wait_ge(T.sem.stored, 16)
+    g.wait_ge(T.sem.stored, 16 * npairs)

from concourse.bass import DstId, RemoteDMATransfer

SCRATCH = {
    "land": ("dram", [8, 128, 8], "float32"),
}
SEMAPHORES = ["loaded", "read", "stored", "pair0", "pair1", "pair2", "pair3"]

ENGINES = 0xFF
NENG = 8


def send_order(core, T, topo):
    n = len(T.cores)
    rank = T.rank_of(core)
    here = topo.chip(core)
    far, near, mate = [], [], []
    for d in range(1, n):
        c = T.cores[(rank + d) % n]
        there = topo.chip(c)
        if topo.mates(here, there):
            mate.append(c)
        elif topo.same_plane(here, there):
            near.append(c)
        else:
            far.append(c)
    return far + near + mate


def rank_program(g, core, T, topo):
    rank = T.rank_of(core)
    if rank is None:
        return
    others = send_order(core, T, topo)
    pair_sem = [T.sem.pair0, T.sem.pair1, T.sem.pair2, T.sem.pair3]
    npairs = len(pair_sem)
    mine = rank // 2
    rows = T.y.shape[0] // npairs

    g.dma_start(T.land[rank], T.x[:]).then_inc(T.sem.loaded, 16)
    g.wait_ge(T.sem.loaded, 16)

    ids = []
    for c in others:
        rid, pid, se = topo.addr(c)
        ids.append(DstId(rid=rid, pnc=pid))
    g.remote_dma_fused(
        [RemoteDMATransfer(dst_ids=ids, dma_engine_mask=ENGINES, remote_sem=pair_sem[mine],
                           srcs=[T.land[rank]], dsts=[T.land[rank] for c in others])],
        local_sem=T.sem.read)

    for k in range(1, npairs + 1):
        p = (mine - k) % npairs
        g.wait_ge(pair_sem[p], NENG if p == mine else 2 * NENG)
        g.dma_start(T.y[p * rows:(p + 1) * rows, :], T.land[2 * p:2 * p + 2]).then_inc(T.sem.stored, 16)
    g.wait_ge(T.sem.read, NENG)
    g.wait_ge(T.sem.stored, 16 * npairs)
